import numpy as np
import ml_dtypes


def mxq(x, axis, fmt="e4m3"):
    dtype, down = {"e4m3": (ml_dtypes.float8_e4m3fn, 7), "e5m2": (ml_dtypes.float8_e5m2, 14)}[fmt]
    v = np.moveaxis(np.asarray(x, np.float32).astype(ml_dtypes.bfloat16).astype(np.float64), axis, -1)
    blocks = v.reshape(v.shape[:-1] + (-1, 32))
    amax = np.abs(blocks).max(-1, keepdims=True)
    byte = np.maximum(np.where(amax > 0, np.frexp(amax)[1] - 1 + 127, 0) - down, 1)
    scale = np.exp2(byte - 127.0)
    codes = (blocks / scale).astype(np.float32).astype(dtype).astype(np.float64)
    return np.moveaxis((codes * scale).reshape(v.shape), -1, axis)


WIDE = False


def mx_kscale(k):
    if not WIDE:
        return np.ones(k)
    levels = np.array([10, -10, 5, -5, 0])
    if k % 512:
        return np.exp2(np.random.permutation(np.resize(levels, k // 32))).repeat(32)
    a = np.empty((k // 512, 16))
    for p in range(k // 512):
        a[p, :8] = np.random.permutation(np.resize(levels, 8))
        for g in range(8):
            far = levels[np.abs(levels - a[p, g]) >= 10]
            a[p, g + 8] = far[np.random.randint(len(far))]
    return np.exp2(a.ravel()).repeat(32)


BF16 = ml_dtypes.bfloat16


def bf(x):
    return np.asarray(x, np.float32).astype(BF16)


def f64(x):
    return np.asarray(x).astype(np.float64)


E2M1 = np.array([0.0, 0.5, 1.0, 1.5, 2.0, 3.0, 4.0, 6.0, -0.0, -0.5, -1.0, -1.5, -2.0, -3.0, -4.0, -6.0])


def pack_weight(w, fmt):
    k, n = w.shape
    w = f64(bf(w)).reshape(k // 32, 32, n)
    amax = np.abs(w).max(1)
    if fmt == "e4m3":
        byte = np.frexp(amax)[1] - 1 + 127 - 7
    else:
        mant, ex = np.frexp(amax / 6.0)
        byte = np.where(mant > 0.5, ex, ex - 1) + 127
    byte = np.clip(np.where(amax > 0, byte, 1), 1, 254)
    scaled = (w * np.exp2(127.0 - byte)[:, None, :]).reshape(k, n).astype(np.float32)
    by_word = np.ascontiguousarray(scaled.reshape(k // 512, 128, 4, n).transpose(0, 1, 3, 2))
    if fmt == "e4m3":
        words = by_word.astype(ml_dtypes.float8_e4m3fn).view(np.uint8)
    else:
        c = by_word.astype(ml_dtypes.float4_e2m1fn).view(np.uint8) & 0xF
        words = c[..., 0::2] | (c[..., 1::2] << 4)
    return np.ascontiguousarray(words), np.ascontiguousarray(byte.astype(np.uint8).reshape(k // 512, 16, n))


def unpack_weight(words, scales, fmt):
    g, p, n, _ = words.shape
    if fmt == "e4m3":
        vals = np.ascontiguousarray(words).view(ml_dtypes.float8_e4m3fn).astype(np.float64)
    else:
        nib = np.empty((g, p, n, 4), np.uint8)
        nib[..., 0::2] = words & 0xF
        nib[..., 1::2] = words >> 4
        vals = E2M1[nib]
    vals = vals * np.repeat(np.exp2(scales.astype(np.float64) - 127.0), 8, axis=1)[..., None]
    return vals.transpose(0, 1, 3, 2).reshape(g * 512, n)
def pack4(w):
    words, scales = pack_weight(w, "e2m1")
    return words.reshape(words.shape[0], 128, -1), scales


def unpack4(words, scales):
    return unpack_weight(words.reshape(words.shape[0], 128, -1, 2), scales, "e2m1")


def planes(Y):
    n, m = Y.shape
    b = f64(bf(Y)).reshape(n // 32, 32, m)
    amax = np.abs(b).max(1)
    byte = np.clip(np.where(amax > 0, np.frexp(amax)[1] - 1 + 127 - 7, 1), 1, 254)
    codes = (b * np.exp2(127.0 - byte)[:, None, :]).reshape(n, m).astype(np.float32).astype(ml_dtypes.float8_e4m3fn).view(np.uint8)
    words = codes.reshape(n // 512, 128, 4, m).transpose(0, 1, 3, 2)
    return np.ascontiguousarray(words), np.ascontiguousarray(byte.astype(np.uint8).reshape(n // 512, 16, m))


T, K, KO, H, DH = 1024, 1536, 512, 4, 512
SCALE = DH ** -0.5


def setup_inputs():
    rn = np.random.randn
    s = mx_kscale(K)
    so = mx_kscale(KO)
    spread = np.exp(0.8 * rn(H * DH))
    x = rn(T, K) * s
    x_outlier = 6.0 * rn(T, KO) * so
    w = 6.0 * rn(K, H * DH) / np.sqrt(K) * spread / s[:, None]
    w_outlier = rn(KO, H * DH) / np.sqrt(KO) * spread / so[:, None]
    w_words, w_scales = pack4(w)
    bias = 0.5 * rn(H, DH) * spread.reshape(H, DH)
    return {"x": bf(x), "w_words": w_words, "w_scales": w_scales,
            "x_outlier": bf(x_outlier), "w_outlier": bf(w_outlier), "bias": bf(bias)}


def reference(x, w_words, w_scales, x_outlier, w_outlier, bias):
    base = mxq(f64(x), 1, "e4m3") @ unpack4(w_words, w_scales)
    extra = mxq(f64(x_outlier), 1, "e4m3") @ mxq(f64(w_outlier), 0, "e4m3")
    y = ((base + extra).reshape(T, H, DH) + f64(bias)) * SCALE
    Y = y.transpose(2, 0, 1).reshape(DH, T * H)
    words, scales = planes(Y)
    return y, words, scales

@@ -1,0 +1,404 @@
+from contextlib import ExitStack
+
+import concourse.mybir as mybir
+from concourse.masks import make_identity
+
+T, K, KO, H, DH = 1024, 1536, 512, 4, 512
+SCALE = DH ** -0.5
+FLOPS = 2 * T * (K + KO) * H * DH
+
+F32 = mybir.dt.float32
+BF16 = mybir.dt.bfloat16
+I32 = mybir.dt.int32
+U32 = mybir.dt.uint32
+U8 = mybir.dt.uint8
+FP8X4 = mybir.dt.float8_e4m3fn_x4
+FP4X4 = mybir.dt.float4_e2m1fn_x4
+ALU = mybir.AluOpType
+
+P = 128
+TILES = T // P
+FP4_PASSES = K // 512
+PASSES = FP4_PASSES + 1
+HEAD_RUNS = [(0, 1), (1, 2), (2, 4)]
+FIRST = 4
+
+
+def tile_outlier_split_query_projection_g5_kernel(
+    tc, x, w_words, w_scales, x_outlier, w_outlier, bias, out_0, out_1, out_2
+):
+    nc = tc.nc
+    y_hbm = out_0.rearrange("t h d -> t (h d)")
+    codes_hbm = out_1[0].rearrange("p m t -> p (m t)").bitcast(I32)
+    scales_hbm = out_2[0].bitcast(I32)
+
+    with ExitStack() as ctx:
+        keep = ctx.enter_context(tc.tile_pool(name="keep", bufs=1))
+        work = ctx.enter_context(tc.tile_pool(name="work", bufs=2))
+        psum = ctx.enter_context(tc.psum_pool(name="psum", bufs=4))
+        ctx.enter_context(tc.manual_schedule())
+
+        ident = keep.tile([P, P], F32, name="ident")
+        make_identity(nc, ident[:])
+
+        x_raw, x_sorted, x_turned, x_codes, x_scales = {}, {}, {}, {}, {}
+        w4, w4_scales, wo_raw, wo_rows, wo_codes, wo_scales = {}, {}, {}, {}, {}, {}
+        w4_planes, y_codes = {}, {}
+        acc, y, y_pairs, y_turned, turn_bank, bias_bank = {}, {}, {}, {}, {}, {}
+
+        bias_words = keep.tile([P, H, 2], F32, name="bias_words")
+        bias_scaled = keep.tile([P, H * DH], F32, name="bias_scaled")
+        y_scales = {}
+        for b in range(TILES // 4):
+            y_scales[b] = keep.tile([P, P * H], U8, name="y_scales%d" % b, align_bytes=64)
+        for h0, h1 in HEAD_RUNS:
+            plane = keep.tile([P, FP4_PASSES, (h1 - h0) * DH], U8, name="w4_scales%d" % h0, align_bytes=64)
+            nc.vector.memset(plane[:].bitcast(I32), 0)
+            for h in range(h0, h1):
+                w4_scales[h] = plane[:, :, (h - h0) * DH : (h - h0 + 1) * DH]
+            w4_planes[h0] = plane
+
+        def load_x(j):
+            x_raw[j] = work.tile([P, K + KO], BF16, name="x_raw", bufs=4)
+            nc.sync.dma_start(out=x_raw[j][:, 0:K], in_=x[j * P : (j + 1) * P, :])
+            nc.sync.dma_start(out=x_raw[j][:, K:], in_=x_outlier[j * P : (j + 1) * P, :])
+
+        def load_w4(h0, h1):
+            words = keep.tile([P, FP4_PASSES, 2 * DH * (h1 - h0)], U8, name="w4_%d" % h0, align_bytes=64)
+            src = w_words[:, :, 2 * DH * h0 : 2 * DH * h1].rearrange("g p n -> p g n")
+            nc.sync.dma_start(out=words[:].bitcast(I32), in_=src.bitcast(I32))
+            for h in range(h0, h1):
+                w4[h] = words[:, :, 2 * DH * (h - h0) : 2 * DH * (h - h0 + 1)]
+            for q in range(4):
+                src = w_scales[:, 4 * q : 4 * q + 4, DH * h0 : DH * h1].rearrange("g r n -> r g n")
+                nc.sync.dma_start(out=w4_planes[h0][32 * q : 32 * q + 4, :, :].bitcast(I32), in_=src.bitcast(I32))
+
+        def load_wo(h0, h1):
+            raw = keep.tile([P, 4, DH * (h1 - h0)], BF16, name="wo_raw%d" % h0)
+            src = w_outlier[:, DH * h0 : DH * h1].rearrange("(p j) n -> p j n", j=4)
+            nc.sync.dma_start(out=raw[:], in_=src)
+            for h in range(h0, h1):
+                wo_raw[h] = raw[:, :, DH * (h - h0) : DH * (h - h0 + 1)]
+
+        def interleave_wo(h, on_vector):
+            wo_rows[h] = work.tile([P, DH, 4], BF16, name="wo_rows", align_bytes=64)
+            dst = wo_rows[h][:].rearrange("p (c i) t -> p c t i", i=4)
+            src = wo_raw[h].rearrange("p t (c i) -> p c t i", i=4)
+            if on_vector:
+                nc.vector.tensor_copy(out=dst, in_=src)
+            else:
+                nc.scalar.copy(out=dst, in_=src)
+
+        def quantize_wo(h):
+            wo_codes[h] = keep.tile([P, DH], U32, name="wo_codes%d" % h, align_bytes=64)
+            wo_scales[h] = keep.tile([P, DH], U8, name="wo_scales%d" % h, align_bytes=64)
+            nc.vector.quantize_mx(
+                out=wo_codes[h][:].bitcast(FP8X4),
+                scales=wo_scales[h][:],
+                in_=wo_rows[h][:].rearrange("p n t -> p (n t)"),
+            )
+
+        def spread_bias(hp):
+            bias_bank[hp] = psum.tile([P, 2, 2, P], F32, name="acc")
+            for hl in range(2):
+                for m in range(2):
+                    col = bias_words[:, 2 * hp + hl, m : m + 1].to_broadcast([P, P])
+                    nc.tensor.transpose(bias_bank[hp][:, hl, m, :], col, ident[:])
+
+        def scale_bias(hp):
+            for hl in range(2):
+                h = 2 * hp + hl
+                src = bias_bank[hp][:, hl, :, :].bitcast(BF16).rearrange("p m (n e) -> p n m e", e=2)
+                dst = bias_scaled[:, DH * h : DH * (h + 1)].rearrange("p (n m e) -> p n m e", m=2, e=2)
+                nc.scalar.mul(out=dst, in_=src, mul=SCALE)
+
+        def sort_x(j):
+            x_sorted[j] = work.tile([P, PASSES, 2, P], F32, name="x_sorted")
+            src = x_raw[j][:].bitcast(F32).rearrange("p (g w u) -> p g u w", g=PASSES, u=2)
+            nc.vector.tensor_copy(out=x_sorted[j][:], in_=src)
+
+        def turn_x(j):
+            words = x_raw[j][:].bitcast(F32)
+            for half in range(2):
+                bank = psum.tile([P, 2, 2, P], F32, name="turn")
+                turn_bank[("x", j, half)] = bank
+                for gl in range(2):
+                    g = 2 * half + gl
+                    for u in range(2):
+                        if j in x_sorted:
+                            src = x_sorted[j][:, g, u, :]
+                        else:
+                            src = words[:, 256 * g + u : 256 * (g + 1) : 2]
+                        nc.tensor.transpose(bank[:, gl, u, :], src, ident[:])
+
+        def copy_x(j, half):
+            if half == 0:
+                x_turned[j] = work.tile([P, PASSES * P * 4], BF16, name="x_turned", bufs=3, align_bytes=64)
+            dst = x_turned[j][:].bitcast(F32).rearrange("p (g i u) -> p g i u", g=PASSES, u=2)
+            src = turn_bank[("x", j, half)][:].rearrange("p g u i -> p g i u")
+            nc.scalar.copy(out=dst[:, 2 * half : 2 * half + 2, :, :], in_=src)
+
+        def quantize_x(j, halves):
+            if j not in x_codes:
+                x_codes[j] = keep.tile([P, PASSES * P], U32, name="x_codes%d" % j, align_bytes=64)
+                x_scales[j] = keep.tile([P, PASSES * P], U8, name="x_scales%d" % j, align_bytes=64)
+            lo, hi = 2 * P * halves[0], 2 * P * (halves[-1] + 1)
+            nc.vector.quantize_mx(
+                out=x_codes[j][:, lo:hi].bitcast(FP8X4),
+                scales=x_scales[j][:, lo:hi],
+                in_=x_turned[j][:, 4 * lo : 4 * hi],
+            )
+
+        def multiply(j, h, passes):
+            for g in passes:
+                if g == 0:
+                    acc[(j, h)] = psum.tile([P, DH], F32, name="acc")
+                if g < FP4_PASSES:
+                    rhs = w4[h][:, g, :].bitcast(FP4X4)
+                    rhs_scale = w4_scales[h][:, g, :]
+                else:
+                    rhs = wo_codes[h][:].bitcast(FP8X4)
+                    rhs_scale = wo_scales[h][:]
+                nc.tensor.matmul_mx(
+                    out=acc[(j, h)][:],
+                    lhsT=x_codes[j][:, g * P : (g + 1) * P].bitcast(FP8X4),
+                    lhsT_scale=x_scales[j][:, g * P : (g + 1) * P],
+                    rhs=rhs,
+                    rhs_scale=rhs_scale,
+                    start=(g == 0),
+                    stop=(g == PASSES - 1),
+                )
+
+        def finish(j, h):
+            if h == 0:
+                y[j] = keep.tile([P, H * DH], F32, name="y%d" % j)
+            cols = slice(DH * h, DH * (h + 1))
+            nc.vector.scalar_tensor_tensor(
+                out=y[j][:, cols], in0=acc[(j, h)][:], scalar=SCALE, in1=bias_scaled[:, cols],
+                op0=ALU.mult, op1=ALU.add,
+            )
+
+        def store_y(j, h0, h1):
+            cols = slice(DH * h0, DH * h1)
+            nc.sync.dma_start(out=y_hbm[j * P : (j + 1) * P, cols], in_=y[j][:, cols])
+
+        def round_y(j, h0, h1, on_vector):
+            hp = h0 // 2
+            if h0 % 2 == 0:
+                y_pairs[(j, hp)] = work.tile([P, 2, 2, P, 2], BF16, name="y_pairs", bufs=8)
+            dst = y_pairs[(j, hp)][:, h0 - 2 * hp : h1 - 2 * hp, :, :, :]
+            src = y[j][:, DH * h0 : DH * h1].rearrange("p (h w u e) -> p h u w e", u=2, e=2, w=P)
+            if on_vector:
+                nc.vector.tensor_copy(out=dst, in_=src)
+            else:
+                nc.scalar.copy(out=dst, in_=src)
+
+        def turn_y(j, h0, h1):
+            hp = h0 // 2
+            if h0 % 2 == 0:
+                turn_bank[("y", j, hp)] = psum.tile([P, 2, 2, P], F32, name="turn")
+            words = y_pairs[(j, hp)][:].rearrange("p h u w e -> p (h u w e)").bitcast(F32)
+            for h in range(h0, h1):
+                for u in range(2):
+                    c = 2 * (h % 2) + u
+                    nc.tensor.transpose(turn_bank[("y", j, hp)][:, h % 2, u, :], words[:, c * P : (c + 1) * P], ident[:])
+
+        def round_y_from_psum(j, h, u):
+            dst = y_pairs[(j, h // 2)][:, h % 2, u, :, :]
+            sums = acc[(j, h)][:].rearrange("p (w u e) -> p u w e", u=2, e=2)
+            row = bias_scaled[:, DH * h : DH * (h + 1)].rearrange("p (w u e) -> p u w e", u=2, e=2)
+            nc.vector.scalar_tensor_tensor(
+                out=dst, in0=sums[:, u, :, :], scalar=SCALE, in1=row[:, u, :, :], op0=ALU.mult, op1=ALU.add
+            )
+            words = y_pairs[(j, h // 2)][:].rearrange("p h u w e -> p (h u w e)").bitcast(F32)
+            c = 2 * (h % 2) + u
+            nc.tensor.transpose(turn_bank[("y", j, h // 2)][:, h % 2, u, :], words[:, c * P : (c + 1) * P], ident[:])
+
+        def copy_y(j, hp, i0=0, i1=P):
+            if j not in y_turned:
+                y_turned[j] = work.tile([P, P * H * 4], BF16, name="y_turned", bufs=5, align_bytes=64)
+            dst = y_turned[j][:].bitcast(F32).rearrange("p (i c) -> p i c", c=8)
+            src = turn_bank[("y", j, hp)][:].rearrange("p h u i -> p i (h u)")
+            nc.scalar.copy(out=dst[:, i0:i1, 4 * hp : 4 * hp + 4], in_=src[:, i0:i1, :])
+
+        def quantize_y(j, i0=0, i1=P):
+            if j not in y_codes:
+                y_codes[j] = work.tile([P, P * H], U32, name="y_codes", bufs=4, align_bytes=64)
+            cols = slice(H * i0, H * i1)
+            nc.vector.quantize_mx(
+                out=y_codes[j][:, cols].bitcast(FP8X4),
+                scales=y_scales[j // 4][4 * (j % 4) : P, cols],
+                in_=y_turned[j][:, 4 * H * i0 : 4 * H * i1],
+            )
+            nc.sync.dma_start(out=codes_hbm[:, H * (P * j + i0) : H * (P * j + i1)], in_=y_codes[j][:, cols].bitcast(I32))
+
+        def store_y_scales(b, queue):
+            rows = y_scales[b][:].bitcast(I32)
+            for q in range(4):
+                dst = scales_hbm[4 * q : 4 * q + 4, 4 * P * b : 4 * P * (b + 1)].rearrange("r (k c) -> k r c", k=4)
+                queue.dma_start(out=dst, in_=rows[32 * q : 32 * q + 16, :])
+
+        nc.sync.dma_start(
+            out=bias_words[:],
+            in_=bias.bitcast(F32).rearrange("h (n m) -> n h m", m=2),
+        )
+        load_x(0)
+        load_w4(0, 1)
+        load_x(1)
+        load_wo(0, 1)
+        load_x(2)
+        load_x(3)
+        load_w4(1, 2)
+        load_wo(1, 2)
+        load_w4(2, 4)
+        load_wo(2, 4)
+
+        fp4, last = [0, 1, 2], [3]
+        spread_bias(0)
+        spread_bias(1)
+        scale_bias(0)
+        turn_x(0)
+        copy_x(0, 0)
+        quantize_x(0, [0])
+        copy_x(0, 1)
+        quantize_x(0, [1])
+        multiply(0, 0, fp4)
+        turn_x(1)
+        copy_x(1, 0)
+        copy_x(1, 1)
+        interleave_wo(0, True)
+        quantize_x(1, [0, 1])
+        quantize_wo(0)
+        turn_x(2)
+        copy_x(2, 0)
+        copy_x(2, 1)
+        multiply(1, 0, fp4)
+        multiply(0, 0, last)
+        multiply(1, 0, last)
+        quantize_x(2, [0, 1])
+        finish(0, 0)
+        finish(1, 0)
+        turn_x(3)
+        copy_x(3, 0)
+        copy_x(3, 1)
+        scale_bias(1)
+        for j in range(FIRST, TILES):
+            load_x(j)
+        multiply(2, 0, fp4 + last)
+        interleave_wo(1, True)
+        quantize_x(3, [0, 1])
+        quantize_wo(1)
+        finish(2, 0)
+        multiply(3, 0, fp4 + last)
+        finish(3, 0)
+
+        interleave_wo(2, False)
+        for j in range(FIRST):
+            multiply(j, 1, fp4 + last)
+            finish(j, 1)
+            store_y(j, 0, 2)
+            if j == 1:
+                quantize_wo(2)
+                interleave_wo(3, False)
+        for j in range(FIRST):
+            multiply(j, 2, fp4 + last)
+            if j == 0:
+                quantize_wo(3)
+            if j in (1, 2):
+                sort_x(FIRST + j - 1)
+            finish(j, 2)
+            round_y(j, 0, 2, False)
+        turn_x(4)
+        turn_x(5)
+        for j in (4, 5):
+            copy_x(j, 0)
+            copy_x(j, 1)
+        for j in range(FIRST):
+            multiply(j, 3, fp4 + last)
+            finish(j, 3)
+            store_y(j, 2, 4)
+            if j in (1, 2):
+                quantize_x(3 + j, [0, 1])
+            if j < 2:
+                round_y(j, 2, 4, False)
+
+        for j in range(FIRST):
+            turn_y(j, 0, 2)
+        for j in range(FIRST):
+            copy_y(j, 0)
+        round_y(2, 2, 4, False)
+        round_y(3, 2, 4, False)
+        for h in range(H):
+            multiply(4, h, fp4 + last)
+            finish(4, h)
+            if h == 0:
+                sort_x(6)
+            if h == 2:
+                round_y(4, 0, 2, True)
+            if h % 2 == 1:
+                store_y(4, h - 1, h + 1)
+
+        for j in (5, 6):
+            a, b = 2 * (j - 5), 2 * (j - 5) + 1
+            turn_x(j + 1)
+            turn_y(a, 2, 4)
+            turn_y(b, 2, 4)
+            copy_x(j + 1, 0)
+            copy_x(j + 1, 1)
+            copy_y(a, 1)
+            copy_y(b, 1)
+            round_y(j - 1, 2, 4, False)
+            for h in range(H):
+                multiply(j, h, fp4 + last)
+                finish(j, h)
+                if h == 0:
+                    if j == 5:
+                        sort_x(7)
+                    quantize_x(j + 1, [0, 1])
+                if h == 1:
+                    quantize_y(a)
+                    round_y(j, 0, 2, False)
+                if h == 2:
+                    quantize_y(b)
+                if h % 2 == 1:
+                    store_y(j, h - 1, h + 1)
+
+        store_y_scales(0, nc.sync)
+
+        for j in (4, 5):
+            turn_y(j, 0, 2)
+            turn_y(j, 2, 4)
+        for j in (4, 5):
+            copy_y(j, 0)
+            copy_y(j, 1)
+        round_y(6, 2, 4, False)
+        multiply(7, 0, fp4 + last)
+        finish(7, 0)
+        quantize_y(4)
+        multiply(7, 1, fp4 + last)
+        finish(7, 1)
+        round_y(7, 0, 2, False)
+        quantize_y(5)
+        store_y(7, 0, 2)
+        multiply(7, 2, fp4 + last)
+        finish(7, 2)
+        store_y(7, 2, 3)
+        turn_y(6, 0, 2)
+        turn_y(6, 2, 4)
+        turn_y(7, 0, 2)
+        copy_y(6, 0)
+        copy_y(6, 1)
+        copy_y(7, 0)
+        round_y(7, 2, 3, True)
+        multiply(7, 3, fp4 + last)
+        turn_y(7, 2, 3)
+        quantize_y(6)
+        round_y_from_psum(7, 3, 0)
+        round_y_from_psum(7, 3, 1)
+        finish(7, 3)
+        store_y(7, 3, 4)
+        for i0 in (0, P // 2):
+            copy_y(7, 1, i0, i0 + P // 2)
+        for i0 in (0, P // 2):
+            quantize_y(7, i0, i0 + P // 2)
+        store_y_scales(1, nc.scalar)

@@ -21,6 +21,7 @@ TILES = T // P
 FP4_PASSES = K // 512
 PASSES = FP4_PASSES + 1
 HEAD_RUNS = [(0, 1), (1, 2), (2, 4)]
+WARM_FIRST, WARM_SECOND = 13, 6
 FIRST = 4
 
 
@@ -46,7 +47,7 @@ def tile_outlier_split_query_projection_g5_kernel(
         w4_planes, y_codes = {}, {}
         acc, y, y_pairs, y_turned, turn_bank, bias_bank = {}, {}, {}, {}, {}, {}
 
-        bias_words = keep.tile([P, H, 2], F32, name="bias_words")
+        bias_words = keep.tile([P, 2, 4], F32, name="bias_words")
         bias_scaled = keep.tile([P, H * DH], F32, name="bias_scaled")
         y_scales = {}
         for b in range(TILES // 4):
@@ -60,7 +61,9 @@ def tile_outlier_split_query_projection_g5_kernel(
 
         def load_x(j):
             x_raw[j] = work.tile([P, K + KO], BF16, name="x_raw", bufs=4)
-            nc.sync.dma_start(out=x_raw[j][:, 0:K], in_=x[j * P : (j + 1) * P, :])
+            cuts = [0, 1024, K] if j == 0 else [0, K]
+            for c0, c1 in zip(cuts, cuts[1:]):
+                nc.sync.dma_start(out=x_raw[j][:, c0:c1], in_=x[j * P : (j + 1) * P, c0:c1])
             nc.sync.dma_start(out=x_raw[j][:, K:], in_=x_outlier[j * P : (j + 1) * P, :])
 
         def load_w4(h0, h1):
@@ -69,6 +72,8 @@ def tile_outlier_split_query_projection_g5_kernel(
             nc.sync.dma_start(out=words[:].bitcast(I32), in_=src.bitcast(I32))
             for h in range(h0, h1):
                 w4[h] = words[:, :, 2 * DH * (h - h0) : 2 * DH * (h - h0 + 1)]
+
+        def load_w4_scales(h0, h1):
             for q in range(4):
                 src = w_scales[:, 4 * q : 4 * q + 4, DH * h0 : DH * h1].rearrange("g r n -> r g n")
                 nc.sync.dma_start(out=w4_planes[h0][32 * q : 32 * q + 4, :, :].bitcast(I32), in_=src.bitcast(I32))
@@ -99,18 +104,15 @@ def tile_outlier_split_query_projection_g5_kernel(
             )
 
         def spread_bias(hp):
-            bias_bank[hp] = psum.tile([P, 2, 2, P], F32, name="acc")
-            for hl in range(2):
-                for m in range(2):
-                    col = bias_words[:, 2 * hp + hl, m : m + 1].to_broadcast([P, P])
-                    nc.tensor.transpose(bias_bank[hp][:, hl, m, :], col, ident[:])
+            bias_bank[hp] = psum.tile([P, 4, P], F32, name="turn")
+            for m in range(4):
+                col = bias_words[:, hp, m : m + 1].to_broadcast([P, P])
+                nc.tensor.transpose(bias_bank[hp][:, m, :], col, ident[:])
 
         def scale_bias(hp):
-            for hl in range(2):
-                h = 2 * hp + hl
-                src = bias_bank[hp][:, hl, :, :].bitcast(BF16).rearrange("p m (n e) -> p n m e", e=2)
-                dst = bias_scaled[:, DH * h : DH * (h + 1)].rearrange("p (n m e) -> p n m e", m=2, e=2)
-                nc.scalar.mul(out=dst, in_=src, mul=SCALE)
+            src = bias_bank[hp][:].bitcast(BF16).rearrange("p m (n e) -> p n m e", e=2)
+            dst = bias_scaled[:, 2 * DH * hp : 2 * DH * (hp + 1)].rearrange("p (n m e) -> p n m e", m=4, e=2)
+            nc.vector.tensor_scalar_mul(dst, src, SCALE)
 
         def sort_x(j):
             x_sorted[j] = work.tile([P, PASSES, 2, P], F32, name="x_sorted")
@@ -238,25 +240,27 @@ def tile_outlier_split_query_projection_g5_kernel(
                 dst = scales_hbm[4 * q : 4 * q + 4, 4 * P * b : 4 * P * (b + 1)].rearrange("r (k c) -> k r c", k=4)
                 queue.dma_start(out=dst, in_=rows[32 * q : 32 * q + 16, :])
 
-        nc.sync.dma_start(
-            out=bias_words[:],
-            in_=bias.bitcast(F32).rearrange("h (n m) -> n h m", m=2),
-        )
         load_x(0)
         load_w4(0, 1)
+        load_w4_scales(0, 1)
         load_x(1)
-        load_wo(0, 1)
         load_x(2)
+        load_wo(0, 1)
+        nc.sync.dma_start(
+            out=bias_words[:],
+            in_=bias.rearrange("h d -> (h d)").bitcast(F32).rearrange("(c n m) -> n c m", c=2, m=4),
+        )
         load_x(3)
         load_w4(1, 2)
+        load_w4_scales(1, 2)
         load_wo(1, 2)
-        load_w4(2, 4)
-        load_wo(2, 4)
+        load_wo(2, 3)
+        load_w4(2, 3)
+        load_w4_scales(2, 4)
+        load_wo(3, 4)
+        load_w4(3, 4)
 
         fp4, last = [0, 1, 2], [3]
-        spread_bias(0)
-        spread_bias(1)
-        scale_bias(0)
         turn_x(0)
         copy_x(0, 0)
         quantize_x(0, [0])
@@ -265,36 +269,40 @@ def tile_outlier_split_query_projection_g5_kernel(
         multiply(0, 0, fp4)
         turn_x(1)
         copy_x(1, 0)
+        quantize_x(1, [0])
         copy_x(1, 1)
-        interleave_wo(0, True)
-        quantize_x(1, [0, 1])
-        quantize_wo(0)
+        quantize_x(1, [1])
         turn_x(2)
         copy_x(2, 0)
         copy_x(2, 1)
         multiply(1, 0, fp4)
-        multiply(0, 0, last)
-        multiply(1, 0, last)
+        interleave_wo(0, True)
         quantize_x(2, [0, 1])
-        finish(0, 0)
-        finish(1, 0)
+        quantize_wo(0)
+        spread_bias(0)
         turn_x(3)
+        spread_bias(1)
+        scale_bias(0)
         copy_x(3, 0)
         copy_x(3, 1)
-        scale_bias(1)
+        interleave_wo(1, False)
         for j in range(FIRST, TILES):
             load_x(j)
-        multiply(2, 0, fp4 + last)
-        interleave_wo(1, True)
+        multiply(2, 0, fp4)
         quantize_x(3, [0, 1])
-        quantize_wo(1)
-        finish(2, 0)
+        for j in range(3):
+            multiply(j, 0, last)
+            finish(j, 0)
         multiply(3, 0, fp4 + last)
         finish(3, 0)
 
+        quantize_wo(1)
+        scale_bias(1)
         interleave_wo(2, False)
+        for j in range(3):
+            multiply(j, 1, fp4)
         for j in range(FIRST):
-            multiply(j, 1, fp4 + last)
+            multiply(j, 1, last if j < 3 else fp4 + last)
             finish(j, 1)
             store_y(j, 0, 2)
             if j == 1:

@@ -308,27 +308,33 @@ def tile_outlier_split_query_projection_g5_kernel(
             if j == 1:
                 quantize_wo(2)
                 interleave_wo(3, False)
+        for j in range(3):
+            multiply(j, 2, fp4)
         for j in range(FIRST):
-            multiply(j, 2, fp4 + last)
-            if j == 0:
-                quantize_wo(3)
-            if j in (1, 2):
-                sort_x(FIRST + j - 1)
+            multiply(j, 2, last if j < 3 else fp4 + last)
             finish(j, 2)
             round_y(j, 0, 2, False)
-        turn_x(4)
-        turn_x(5)
-        for j in (4, 5):
-            copy_x(j, 0)
-            copy_x(j, 1)
+            if j == 1:
+                sort_x(4)
+            if j == 2:
+                quantize_wo(3)
+        sort_x(5)
+        for j in range(2):
+            multiply(j, 3, fp4)
         for j in range(FIRST):
-            multiply(j, 3, fp4 + last)
+            if j == 2:
+                turn_x(4)
+                turn_x(5)
+                for jj in (4, 5):
+                    copy_x(jj, 0)
+                    copy_x(jj, 1)
+            multiply(j, 3, last if j < 2 else fp4 + last)
             finish(j, 3)
             store_y(j, 2, 4)
-            if j in (1, 2):
-                quantize_x(3 + j, [0, 1])
-            if j < 2:
-                round_y(j, 2, 4, False)
+            if j >= 2:
+                quantize_x(2 + j, [0, 1])
+        round_y(0, 2, 4, False)
+        round_y(1, 2, 4, False)
 
         for j in range(FIRST):
             turn_y(j, 0, 2)
@@ -368,6 +374,8 @@ def tile_outlier_split_query_projection_g5_kernel(
                     round_y(j, 0, 2, False)
                 if h == 2:
                     quantize_y(b)
+                    if j == 6:
+                        round_y(6, 2, 3, False)
                 if h % 2 == 1:
                     store_y(j, h - 1, h + 1)
 
@@ -376,31 +384,34 @@ def tile_outlier_split_query_projection_g5_kernel(
         for j in (4, 5):
             turn_y(j, 0, 2)
             turn_y(j, 2, 4)
-        for j in (4, 5):
-            copy_y(j, 0)
-            copy_y(j, 1)
-        round_y(6, 2, 4, False)
+        copy_y(4, 0)
+        round_y(6, 3, 4, False)
+        copy_y(5, 0)
+        copy_y(4, 1)
+        copy_y(5, 1)
         multiply(7, 0, fp4 + last)
         finish(7, 0)
         quantize_y(4)
+        round_y(7, 0, 1, False)
+        store_y(7, 0, 1)
         multiply(7, 1, fp4 + last)
         finish(7, 1)
-        round_y(7, 0, 2, False)
+        store_y(7, 1, 2)
         quantize_y(5)
-        store_y(7, 0, 2)
-        multiply(7, 2, fp4 + last)
-        finish(7, 2)
-        store_y(7, 2, 3)
         turn_y(6, 0, 2)
         turn_y(6, 2, 4)
-        turn_y(7, 0, 2)
         copy_y(6, 0)
         copy_y(6, 1)
-        copy_y(7, 0)
-        round_y(7, 2, 3, True)
-        multiply(7, 3, fp4 + last)
-        turn_y(7, 2, 3)
+        round_y(7, 1, 2, False)
+        multiply(7, 2, fp4 + last)
+        finish(7, 2)
+        round_y(7, 2, 3, False)
+        store_y(7, 2, 3)
         quantize_y(6)
+        multiply(7, 3, fp4 + last)
+        turn_y(7, 0, 2)
+        turn_y(7, 2, 3)
+        copy_y(7, 0)
         round_y_from_psum(7, 3, 0)
         round_y_from_psum(7, 3, 1)
         finish(7, 3)

from contextlib import ExitStack

import concourse.mybir as mybir
from concourse.masks import make_identity

T, K, KO, H, DH = 1024, 1536, 512, 4, 512
SCALE = DH ** -0.5
FLOPS = 2 * T * (K + KO) * H * DH

F32 = mybir.dt.float32
BF16 = mybir.dt.bfloat16
I32 = mybir.dt.int32
U32 = mybir.dt.uint32
U8 = mybir.dt.uint8
FP8X4 = mybir.dt.float8_e4m3fn_x4
FP4X4 = mybir.dt.float4_e2m1fn_x4
ALU = mybir.AluOpType

P = 128
TILES = T // P
FP4_PASSES = K // 512
PASSES = FP4_PASSES + 1
HEAD_RUNS = [(0, 1), (1, 2), (2, 4)]
WARM_FIRST, WARM_SECOND = 13, 6
FIRST = 4


def tile_outlier_split_query_projection_g5_kernel(
    tc, x, w_words, w_scales, x_outlier, w_outlier, bias, out_0, out_1, out_2
):
    nc = tc.nc
    y_hbm = out_0.rearrange("t h d -> t (h d)")
    codes_hbm = out_1[0].rearrange("p m t -> p (m t)").bitcast(I32)
    scales_hbm = out_2[0].bitcast(I32)

    with ExitStack() as ctx:
        keep = ctx.enter_context(tc.tile_pool(name="keep", bufs=1))
        work = ctx.enter_context(tc.tile_pool(name="work", bufs=2))
        psum = ctx.enter_context(tc.psum_pool(name="psum", bufs=4))
        ctx.enter_context(tc.manual_schedule())

        ident = keep.tile([P, P], F32, name="ident")
        make_identity(nc, ident[:])

        x_raw, x_sorted, x_turned, x_codes, x_scales = {}, {}, {}, {}, {}
        w4, w4_scales, wo_raw, wo_rows, wo_codes, wo_scales = {}, {}, {}, {}, {}, {}
        w4_planes, y_codes = {}, {}
        acc, y, y_pairs, y_turned, turn_bank, bias_bank = {}, {}, {}, {}, {}, {}

        bias_words = keep.tile([P, 2, 4], F32, name="bias_words")
        bias_scaled = keep.tile([P, H * DH], F32, name="bias_scaled")
        y_scales = {}
        for b in range(TILES // 4):
            y_scales[b] = keep.tile([P, P * H], U8, name="y_scales%d" % b, align_bytes=64)
        for h0, h1 in HEAD_RUNS:
            plane = keep.tile([P, FP4_PASSES, (h1 - h0) * DH], U8, name="w4_scales%d" % h0, align_bytes=64)
            nc.vector.memset(plane[:].bitcast(I32), 0)
            for h in range(h0, h1):
                w4_scales[h] = plane[:, :, (h - h0) * DH : (h - h0 + 1) * DH]
            w4_planes[h0] = plane

        def load_x(j):
            x_raw[j] = work.tile([P, K + KO], BF16, name="x_raw", bufs=4)
            cuts = [0, 1024, K] if j == 0 else [0, K]
            for c0, c1 in zip(cuts, cuts[1:]):
                nc.sync.dma_start(out=x_raw[j][:, c0:c1], in_=x[j * P : (j + 1) * P, c0:c1])
            nc.sync.dma_start(out=x_raw[j][:, K:], in_=x_outlier[j * P : (j + 1) * P, :])

        def load_w4(h0, h1):
            words = keep.tile([P, FP4_PASSES, 2 * DH * (h1 - h0)], U8, name="w4_%d" % h0, align_bytes=64)
            src = w_words[:, :, 2 * DH * h0 : 2 * DH * h1].rearrange("g p n -> p g n")
            nc.sync.dma_start(out=words[:].bitcast(I32), in_=src.bitcast(I32))
            for h in range(h0, h1):
                w4[h] = words[:, :, 2 * DH * (h - h0) : 2 * DH * (h - h0 + 1)]

        def load_w4_scales(h0, h1):
            for q in range(4):
                src = w_scales[:, 4 * q : 4 * q + 4, DH * h0 : DH * h1].rearrange("g r n -> r g n")
                nc.sync.dma_start(out=w4_planes[h0][32 * q : 32 * q + 4, :, :].bitcast(I32), in_=src.bitcast(I32))

        def load_wo(h0, h1):
            raw = keep.tile([P, 4, DH * (h1 - h0)], BF16, name="wo_raw%d" % h0)
            src = w_outlier[:, DH * h0 : DH * h1].rearrange("(p j) n -> p j n", j=4)
            nc.sync.dma_start(out=raw[:], in_=src)
            for h in range(h0, h1):
                wo_raw[h] = raw[:, :, DH * (h - h0) : DH * (h - h0 + 1)]

        def interleave_wo(h, on_vector):
            wo_rows[h] = work.tile([P, DH, 4], BF16, name="wo_rows", align_bytes=64)
            dst = wo_rows[h][:].rearrange("p (c i) t -> p c t i", i=4)
            src = wo_raw[h].rearrange("p t (c i) -> p c t i", i=4)
            if on_vector:
                nc.vector.tensor_copy(out=dst, in_=src)
            else:
                nc.scalar.copy(out=dst, in_=src)

        def quantize_wo(h):
            wo_codes[h] = keep.tile([P, DH], U32, name="wo_codes%d" % h, align_bytes=64)
            wo_scales[h] = keep.tile([P, DH], U8, name="wo_scales%d" % h, align_bytes=64)
            nc.vector.quantize_mx(
                out=wo_codes[h][:].bitcast(FP8X4),
                scales=wo_scales[h][:],
                in_=wo_rows[h][:].rearrange("p n t -> p (n t)"),
            )

        def spread_bias(hp):
            bias_bank[hp] = psum.tile([P, 4, P], F32, name="turn")
            for m in range(4):
                col = bias_words[:, hp, m : m + 1].to_broadcast([P, P])
                nc.tensor.transpose(bias_bank[hp][:, m, :], col, ident[:])

        def scale_bias(hp):
            src = bias_bank[hp][:].bitcast(BF16).rearrange("p m (n e) -> p n m e", e=2)
            dst = bias_scaled[:, 2 * DH * hp : 2 * DH * (hp + 1)].rearrange("p (n m e) -> p n m e", m=4, e=2)
            nc.vector.tensor_scalar_mul(dst, src, SCALE)

        def sort_x(j):
            x_sorted[j] = work.tile([P, PASSES, 2, P], F32, name="x_sorted")
            src = x_raw[j][:].bitcast(F32).rearrange("p (g w u) -> p g u w", g=PASSES, u=2)
            nc.vector.tensor_copy(out=x_sorted[j][:], in_=src)

        def turn_x(j):
            words = x_raw[j][:].bitcast(F32)
            for half in range(2):
                bank = psum.tile([P, 2, 2, P], F32, name="turn")
                turn_bank[("x", j, half)] = bank
                for gl in range(2):
                    g = 2 * half + gl
                    for u in range(2):
                        if j in x_sorted:
                            src = x_sorted[j][:, g, u, :]
                        else:
                            src = words[:, 256 * g + u : 256 * (g + 1) : 2]
                        nc.tensor.transpose(bank[:, gl, u, :], src, ident[:])

        def copy_x(j, half):
            if half == 0:
                x_turned[j] = work.tile([P, PASSES * P * 4], BF16, name="x_turned", bufs=3, align_bytes=64)
            dst = x_turned[j][:].bitcast(F32).rearrange("p (g i u) -> p g i u", g=PASSES, u=2)
            src = turn_bank[("x", j, half)][:].rearrange("p g u i -> p g i u")
            nc.scalar.copy(out=dst[:, 2 * half : 2 * half + 2, :, :], in_=src)

        def quantize_x(j, halves):
            if j not in x_codes:
                x_codes[j] = keep.tile([P, PASSES * P], U32, name="x_codes%d" % j, align_bytes=64)
                x_scales[j] = keep.tile([P, PASSES * P], U8, name="x_scales%d" % j, align_bytes=64)
            lo, hi = 2 * P * halves[0], 2 * P * (halves[-1] + 1)
            nc.vector.quantize_mx(
                out=x_codes[j][:, lo:hi].bitcast(FP8X4),
                scales=x_scales[j][:, lo:hi],
                in_=x_turned[j][:, 4 * lo : 4 * hi],
            )

        def multiply(j, h, passes):
            for g in passes:
                if g == 0:
                    acc[(j, h)] = psum.tile([P, DH], F32, name="acc")
                if g < FP4_PASSES:
                    rhs = w4[h][:, g, :].bitcast(FP4X4)
                    rhs_scale = w4_scales[h][:, g, :]
                else:
                    rhs = wo_codes[h][:].bitcast(FP8X4)
                    rhs_scale = wo_scales[h][:]
                nc.tensor.matmul_mx(
                    out=acc[(j, h)][:],
                    lhsT=x_codes[j][:, g * P : (g + 1) * P].bitcast(FP8X4),
                    lhsT_scale=x_scales[j][:, g * P : (g + 1) * P],
                    rhs=rhs,
                    rhs_scale=rhs_scale,
                    start=(g == 0),
                    stop=(g == PASSES - 1),
                )

        def finish(j, h):
            if h == 0:
                y[j] = keep.tile([P, H * DH], F32, name="y%d" % j)
            cols = slice(DH * h, DH * (h + 1))
            nc.vector.scalar_tensor_tensor(
                out=y[j][:, cols], in0=acc[(j, h)][:], scalar=SCALE, in1=bias_scaled[:, cols],
                op0=ALU.mult, op1=ALU.add,
            )

        def store_y(j, h0, h1):
            cols = slice(DH * h0, DH * h1)
            nc.sync.dma_start(out=y_hbm[j * P : (j + 1) * P, cols], in_=y[j][:, cols])

        def round_y(j, h0, h1, on_vector):
            hp = h0 // 2
            if h0 % 2 == 0:
                y_pairs[(j, hp)] = work.tile([P, 2, 2, P, 2], BF16, name="y_pairs", bufs=8)
            dst = y_pairs[(j, hp)][:, h0 - 2 * hp : h1 - 2 * hp, :, :, :]
            src = y[j][:, DH * h0 : DH * h1].rearrange("p (h w u e) -> p h u w e", u=2, e=2, w=P)
            if on_vector:
                nc.vector.tensor_copy(out=dst, in_=src)
            else:
                nc.scalar.copy(out=dst, in_=src)

        def turn_y(j, h0, h1):
            hp = h0 // 2
            if h0 % 2 == 0:
                turn_bank[("y", j, hp)] = psum.tile([P, 2, 2, P], F32, name="turn")
            words = y_pairs[(j, hp)][:].rearrange("p h u w e -> p (h u w e)").bitcast(F32)
            for h in range(h0, h1):
                for u in range(2):
                    c = 2 * (h % 2) + u
                    nc.tensor.transpose(turn_bank[("y", j, hp)][:, h % 2, u, :], words[:, c * P : (c + 1) * P], ident[:])

        def round_y_from_psum(j, h, u):
            dst = y_pairs[(j, h // 2)][:, h % 2, u, :, :]
            sums = acc[(j, h)][:].rearrange("p (w u e) -> p u w e", u=2, e=2)
            row = bias_scaled[:, DH * h : DH * (h + 1)].rearrange("p (w u e) -> p u w e", u=2, e=2)
            nc.vector.scalar_tensor_tensor(
                out=dst, in0=sums[:, u, :, :], scalar=SCALE, in1=row[:, u, :, :], op0=ALU.mult, op1=ALU.add
            )
            words = y_pairs[(j, h // 2)][:].rearrange("p h u w e -> p (h u w e)").bitcast(F32)
            c = 2 * (h % 2) + u
            nc.tensor.transpose(turn_bank[("y", j, h // 2)][:, h % 2, u, :], words[:, c * P : (c + 1) * P], ident[:])

        def copy_y(j, hp, i0=0, i1=P):
            if j not in y_turned:
                y_turned[j] = work.tile([P, P * H * 4], BF16, name="y_turned", bufs=5, align_bytes=64)
            dst = y_turned[j][:].bitcast(F32).rearrange("p (i c) -> p i c", c=8)
            src = turn_bank[("y", j, hp)][:].rearrange("p h u i -> p i (h u)")
            nc.scalar.copy(out=dst[:, i0:i1, 4 * hp : 4 * hp + 4], in_=src[:, i0:i1, :])

        def quantize_y(j, i0=0, i1=P):
            if j not in y_codes:
                y_codes[j] = work.tile([P, P * H], U32, name="y_codes", bufs=4, align_bytes=64)
            cols = slice(H * i0, H * i1)
            nc.vector.quantize_mx(
                out=y_codes[j][:, cols].bitcast(FP8X4),
                scales=y_scales[j // 4][4 * (j % 4) : P, cols],
                in_=y_turned[j][:, 4 * H * i0 : 4 * H * i1],
            )
            nc.sync.dma_start(out=codes_hbm[:, H * (P * j + i0) : H * (P * j + i1)], in_=y_codes[j][:, cols].bitcast(I32))

        def store_y_scales(b, queue):
            rows = y_scales[b][:].bitcast(I32)
            for q in range(4):
                dst = scales_hbm[4 * q : 4 * q + 4, 4 * P * b : 4 * P * (b + 1)].rearrange("r (k c) -> k r c", k=4)
                queue.dma_start(out=dst, in_=rows[32 * q : 32 * q + 16, :])

        load_x(0)
        load_w4(0, 1)
        load_w4_scales(0, 1)
        load_x(1)
        load_x(2)
        load_wo(0, 1)
        nc.sync.dma_start(
            out=bias_words[:],
            in_=bias.rearrange("h d -> (h d)").bitcast(F32).rearrange("(c n m) -> n c m", c=2, m=4),
        )
        load_x(3)
        load_w4(1, 2)
        load_w4_scales(1, 2)
        load_wo(1, 2)
        load_wo(2, 3)
        load_w4(2, 3)
        load_w4_scales(2, 4)
        load_wo(3, 4)
        load_w4(3, 4)

        fp4, last = [0, 1, 2], [3]
        turn_x(0)
        copy_x(0, 0)
        quantize_x(0, [0])
        copy_x(0, 1)
        quantize_x(0, [1])
        multiply(0, 0, fp4)
        turn_x(1)
        copy_x(1, 0)
        quantize_x(1, [0])
        copy_x(1, 1)
        quantize_x(1, [1])
        turn_x(2)
        copy_x(2, 0)
        copy_x(2, 1)
        multiply(1, 0, fp4)
        interleave_wo(0, True)
        quantize_x(2, [0, 1])
        quantize_wo(0)
        spread_bias(0)
        turn_x(3)
        spread_bias(1)
        scale_bias(0)
        copy_x(3, 0)
        copy_x(3, 1)
        interleave_wo(1, False)
        for j in range(FIRST, TILES):
            load_x(j)
        multiply(2, 0, fp4)
        quantize_x(3, [0, 1])
        for j in range(3):
            multiply(j, 0, last)
            finish(j, 0)
        multiply(3, 0, fp4 + last)
        finish(3, 0)

        quantize_wo(1)
        scale_bias(1)
        interleave_wo(2, False)
        for j in range(3):
            multiply(j, 1, fp4)
        for j in range(FIRST):
            multiply(j, 1, last if j < 3 else fp4 + last)
            finish(j, 1)
            store_y(j, 0, 2)
            if j == 1:
                quantize_wo(2)
                interleave_wo(3, False)
        for j in range(3):
            multiply(j, 2, fp4)
        for j in range(FIRST):
            multiply(j, 2, last if j < 3 else fp4 + last)
            finish(j, 2)
            round_y(j, 0, 2, False)
            if j == 1:
                sort_x(4)
            if j == 2:
                quantize_wo(3)
        sort_x(5)
        for j in range(2):
            multiply(j, 3, fp4)
        for j in range(FIRST):
            if j == 2:
                turn_x(4)
                turn_x(5)
                for jj in (4, 5):
                    copy_x(jj, 0)
                    copy_x(jj, 1)
            multiply(j, 3, last if j < 2 else fp4 + last)
            finish(j, 3)
            store_y(j, 2, 4)
            if j >= 2:
                quantize_x(2 + j, [0, 1])
        round_y(0, 2, 4, False)
        round_y(1, 2, 4, False)

        for j in range(FIRST):
            turn_y(j, 0, 2)
        for j in range(FIRST):
            copy_y(j, 0)
        round_y(2, 2, 4, False)
        round_y(3, 2, 4, False)
        for h in range(H):
            multiply(4, h, fp4 + last)
            finish(4, h)
            if h == 0:
                sort_x(6)
            if h == 2:
                round_y(4, 0, 2, True)
            if h % 2 == 1:
                store_y(4, h - 1, h + 1)

        for j in (5, 6):
            a, b = 2 * (j - 5), 2 * (j - 5) + 1
            turn_x(j + 1)
            turn_y(a, 2, 4)
            turn_y(b, 2, 4)
            copy_x(j + 1, 0)
            copy_x(j + 1, 1)
            copy_y(a, 1)
            copy_y(b, 1)
            round_y(j - 1, 2, 4, False)
            for h in range(H):
                multiply(j, h, fp4 + last)
                finish(j, h)
                if h == 0:
                    if j == 5:
                        sort_x(7)
                    quantize_x(j + 1, [0, 1])
                if h == 1:
                    quantize_y(a)
                    round_y(j, 0, 2, False)
                if h == 2:
                    quantize_y(b)
                    if j == 6:
                        round_y(6, 2, 3, False)
                if h % 2 == 1:
                    store_y(j, h - 1, h + 1)

        store_y_scales(0, nc.sync)

        for j in (4, 5):
            turn_y(j, 0, 2)
            turn_y(j, 2, 4)
        copy_y(4, 0)
        round_y(6, 3, 4, False)
        copy_y(5, 0)
        copy_y(4, 1)
        copy_y(5, 1)
        multiply(7, 0, fp4 + last)
        finish(7, 0)
        quantize_y(4)
        round_y(7, 0, 1, False)
        store_y(7, 0, 1)
        multiply(7, 1, fp4 + last)
        finish(7, 1)
        store_y(7, 1, 2)
        quantize_y(5)
        turn_y(6, 0, 2)
        turn_y(6, 2, 4)
        copy_y(6, 0)
        copy_y(6, 1)
        round_y(7, 1, 2, False)
        multiply(7, 2, fp4 + last)
        finish(7, 2)
        round_y(7, 2, 3, False)
        store_y(7, 2, 3)
        quantize_y(6)
        multiply(7, 3, fp4 + last)
        turn_y(7, 0, 2)
        turn_y(7, 2, 3)
        copy_y(7, 0)
        round_y_from_psum(7, 3, 0)
        round_y_from_psum(7, 3, 1)
        finish(7, 3)
        store_y(7, 3, 4)
        for i0 in (0, P // 2):
            copy_y(7, 1, i0, i0 + P // 2)
        for i0 in (0, P // 2):
            quantize_y(7, i0, i0 + P // 2)
        store_y_scales(1, nc.scalar)
